import numpy as np
import ml_dtypes


def mxq(x, axis, fmt="e4m3"):
    dtype, down = {"e4m3": (ml_dtypes.float8_e4m3fn, 7), "e5m2": (ml_dtypes.float8_e5m2, 14)}[fmt]
    v = np.moveaxis(np.asarray(x, np.float32).astype(ml_dtypes.bfloat16).astype(np.float64), axis, -1)
    blocks = v.reshape(v.shape[:-1] + (-1, 32))
    amax = np.abs(blocks).max(-1, keepdims=True)
    byte = np.maximum(np.where(amax > 0, np.frexp(amax)[1] - 1 + 127, 0) - down, 1)
    scale = np.exp2(byte - 127.0)
    codes = (blocks / scale).astype(np.float32).astype(dtype).astype(np.float64)
    return np.moveaxis((codes * scale).reshape(v.shape), -1, axis)


WIDE = False


def mx_kscale(k):
    if not WIDE:
        return np.ones(k)
    levels = np.array([10, -10, 5, -5, 0])
    if k % 512:
        return np.exp2(np.random.permutation(np.resize(levels, k // 32))).repeat(32)
    a = np.empty((k // 512, 16))
    for p in range(k // 512):
        a[p, :8] = np.random.permutation(np.resize(levels, 8))
        for g in range(8):
            far = levels[np.abs(levels - a[p, g]) >= 10]
            a[p, g + 8] = far[np.random.randint(len(far))]
    return np.exp2(a.ravel()).repeat(32)


BF16 = ml_dtypes.bfloat16


def bf(x):
    return np.asarray(x, np.float32).astype(BF16)


def f64(x):
    return np.asarray(x).astype(np.float64)


E2M1 = np.array([0.0, 0.5, 1.0, 1.5, 2.0, 3.0, 4.0, 6.0, -0.0, -0.5, -1.0, -1.5, -2.0, -3.0, -4.0, -6.0])


def pack_weight(w, fmt):
    k, n = w.shape
    w = f64(bf(w)).reshape(k // 32, 32, n)
    amax = np.abs(w).max(1)
    if fmt == "e4m3":
        byte = np.frexp(amax)[1] - 1 + 127 - 7
    else:
        mant, ex = np.frexp(amax / 6.0)
        byte = np.where(mant > 0.5, ex, ex - 1) + 127
    byte = np.clip(np.where(amax > 0, byte, 1), 1, 254)
    scaled = (w * np.exp2(127.0 - byte)[:, None, :]).reshape(k, n).astype(np.float32)
    by_word = np.ascontiguousarray(scaled.reshape(k // 512, 128, 4, n).transpose(0, 1, 3, 2))
    if fmt == "e4m3":
        words = by_word.astype(ml_dtypes.float8_e4m3fn).view(np.uint8)
    else:
        c = by_word.astype(ml_dtypes.float4_e2m1fn).view(np.uint8) & 0xF
        words = c[..., 0::2] | (c[..., 1::2] << 4)
    return np.ascontiguousarray(words), np.ascontiguousarray(byte.astype(np.uint8).reshape(k // 512, 16, n))


def unpack_weight(words, scales, fmt):
    g, p, n, _ = words.shape
    if fmt == "e4m3":
        vals = np.ascontiguousarray(words).view(ml_dtypes.float8_e4m3fn).astype(np.float64)
    else:
        nib = np.empty((g, p, n, 4), np.uint8)
        nib[..., 0::2] = words & 0xF
        nib[..., 1::2] = words >> 4
        vals = E2M1[nib]
    vals = vals * np.repeat(np.exp2(scales.astype(np.float64) - 127.0), 8, axis=1)[..., None]
    return vals.transpose(0, 1, 3, 2).reshape(g * 512, n)
def pack4(w):
    words, scales = pack_weight(w, "e2m1")
    return words.reshape(words.shape[0], 128, -1), scales


def unpack4(words, scales):
    return unpack_weight(words.reshape(words.shape[0], 128, -1, 2), scales, "e2m1")


N, D, F, R = 1024, 1024, 1024, 512


def draw0():
    s = mx_kscale(D)
    u = mx_kscale(R)
    v = mx_kscale(R)
    x = bf(np.random.standard_normal((N, D)) * s)
    w0_words, w0_scales = pack4(np.random.standard_normal((D, F)) / np.sqrt(D) / s[:, None])
    a_words, a_scales = pack4(np.random.standard_normal((D, R)) / np.sqrt(D) / s[:, None])
    d = bf((1.0 + 0.1 * np.random.standard_normal(R)) * v)
    m = np.random.standard_normal((R, R)) / np.sqrt(R) * u[None, :] / v[:, None]
    m_words, m_scales = pack4(np.ascontiguousarray(m.T))
    bu_words, bu_scales = pack4(np.random.standard_normal((R, F)) / u[:, None])
    return {
        "x": x,
        "w0_words": w0_words,
        "w0_scales": w0_scales,
        "a_words": a_words,
        "a_scales": a_scales,
        "d": d,
        "m_words": m_words,
        "m_scales": m_scales,
        "bu_words": bu_words,
        "bu_scales": bu_scales,
    }


def core(x, w0_words, w0_scales, a_words, a_scales, d, m_words, m_scales, bu_words, bu_scales):
    rank = d.shape[0]
    xq = mxq(f64(x), 1, "e4m3")
    base = xq @ unpack4(w0_words, w0_scales)
    p = xq @ unpack4(a_words, a_scales)
    pg = p * f64(d)[None, :]
    c = unpack4(m_words, m_scales).T @ unpack4(bu_words, bu_scales)
    t = mxq(pg, 1, "e4m3") @ mxq(c, 0, "e4m3")
    return base + t / np.sqrt(rank)


def e4m3fn_bytes(y):
    return np.clip(np.asarray(y, np.float64), -448.0, 448.0).astype(np.float32).astype(ml_dtypes.float8_e4m3fn).view(np.uint8)


def e4m3fn_values(b):
    return np.asarray(b, np.uint8).view(ml_dtypes.float8_e4m3fn).astype(np.float64)


def setup_inputs():
    d = draw0()
    x0 = np.asarray(d['x']).astype(np.float64)
    s = (np.max(np.abs(x0), axis=(0,), keepdims=True) / 448.0).astype(np.float32)
    out = {}
    for k, v in d.items():
        if k == 'x':
            out['x_bytes'] = e4m3fn_bytes(x0 / s.astype(np.float64))
            out['x_scale'] = s
        else:
            out[k] = v
    return out


def reference(x_bytes, x_scale, w0_words, w0_scales, a_words, a_scales, d, m_words, m_scales, bu_words, bu_scales):
    return core(e4m3fn_values(x_bytes) * x_scale.astype(np.float64), w0_words, w0_scales, a_words, a_scales, d, m_words, m_scales, bu_words, bu_scales)

@@ -1,0 +1,480 @@
+import math
+from contextlib import ExitStack
+
+import concourse.mybir as mybir
+from concourse.masks import make_identity
+
+N, D, F, R = 1024, 1024, 1024, 512
+FLOPS = 2 * N * D * F + 2 * N * D * R + 2 * R * R * F + 2 * N * R * F
+
+F32 = mybir.dt.float32
+BF16 = mybir.dt.bfloat16
+I32 = mybir.dt.int32
+U32 = mybir.dt.uint32
+U8 = mybir.dt.uint8
+FP8 = mybir.dt.float8_e4m3fn
+FP8X4 = mybir.dt.float8_e4m3fn_x4
+FP4X4 = mybir.dt.float4_e2m1fn_x4
+ALU = mybir.AluOpType
+ACT = mybir.ActivationFunctionType
+
+P = 128
+PACK = 4
+BANK = 512
+TILES = N // P
+PASSES = D // BANK
+
+
+def tile_moslorasubspacemixerrankgain_w4_kernel(
+    tc, x_bytes, x_scale, w0_words, w0_scales, a_words, a_scales, d, m_words, m_scales, bu_words, bu_scales, out
+):
+    nc = tc.nc
+    with ExitStack() as ctx:
+        keep = ctx.enter_context(tc.tile_pool(name="keep", bufs=1))
+        psum = ctx.enter_context(tc.psum_pool(name="psum", bufs=8))
+        ctx.enter_context(tc.manual_schedule())
+
+        def sb(name, cols, dtype, rows=P):
+            return keep.tile([rows, cols], dtype, name=name, align_bytes=64)
+
+        hbm_words = {"w0": w0_words, "a": a_words, "m": m_words, "bu": bu_words}
+        hbm_scales = {"w0": w0_scales, "a": a_scales, "m": m_scales, "bu": bu_scales}
+        scales = {w: sb(w + "_scale_rows", s.shape[0] * s.shape[2], U8) for w, s in hbm_scales.items()}
+        words = {w: sb(w + "_code_words", hbm_words[w].shape[0] * hbm_words[w].shape[2], U8) for w in ("a", "m", "bu")}
+        w0_pass = [sb("w0_code_words_%d" % g, 2 * F, U8) for g in range(PASSES)]
+        sliced_words = {w: sb(w + "_sliced_words", words[w].shape[1], U8) for w in ("a", "m")}
+        sliced_scales = {w: sb(w + "_sliced_scales", scales[w].shape[1], U8) for w in ("a", "m")}
+
+        ident = sb("ident", P, F32)
+        gain_rows = sb("gain_rows", P, BF16, rows=PACK)
+        gain_square = sb("gain_square", P, F32)
+        gain = sb("gain", PACK, F32)
+        x_scale_cols = sb("x_scale_cols", PASSES * PACK, F32)
+        x_scale_spread = sb("x_scale_spread", D, F32)
+
+        x_rows = x_bytes.rearrange("(h p j) k -> h p (j k)", p=P, j=2)
+        out_rows = out.rearrange("(h p j) f -> h j p f", p=P, j=2)
+        x_raw = {}
+        x_wide = [sb("x_wide_%d" % j, D, BF16) for j in range(TILES)]
+        x_turned = [sb("x_turned_%d" % j, D, BF16) for j in range(TILES)]
+        x_codes = {(c, g): sb("x_codes_%d_%d" % (c, g), BANK, U32) for c in range(2) for g in range(PASSES)}
+        x_scales = {(c, g): sb("x_scales_%d_%d" % (c, g), BANK, U8) for c in range(2) for g in range(PASSES)}
+        pg_planes = [sb("pg_planes_%d" % c, PACK * BANK, BF16) for c in range(2)]
+        pg_woven = [sb("pg_woven_%d" % c, PACK * BANK, BF16) for c in range(2)]
+        pg_codes = [sb("pg_codes_%d" % c, BANK, U32) for c in range(2)]
+        pg_scales = [sb("pg_scales_%d" % c, BANK, U8) for c in range(2)]
+        c_planes = [sb("c_planes_%d" % h, PACK * BANK, BF16) for h in range(2)]
+        c_woven = [sb("c_woven_%d" % h, PACK * BANK, BF16) for h in range(2)]
+        c_codes = [sb("c_codes_%d" % h, BANK, U32) for h in range(2)]
+        c_scales = [sb("c_scales_%d" % h, BANK, U8) for h in range(2)]
+        result = {(j, h): sb("result_%d_%d" % (j, h), BANK, F32) for j in range(TILES) for h in range(2)}
+        banks = {}
+
+        def new_bank(*key):
+            banks[key] = psum.tile([P, BANK], F32, name="bank", tag="bank")
+            return banks[key]
+
+        on_vector = nc.vector.tensor_copy
+        on_scalar = nc.scalar.copy
+
+        def on_scalar_act(out, in_):
+            nc.scalar.activation(out=out, in_=in_, func=ACT.Copy)
+
+        def clear_scales(w):
+            nc.vector.memset(scales[w][:].bitcast(I32), 0)
+
+        def setup():
+            make_identity(nc, ident[:])
+            nc.gpsimd.memset(gain_square[:], 0.0)
+
+        def load_x_scale():
+            nc.sync.dma_start(
+                out=x_scale_cols[:].rearrange("p (g t) -> p g t", t=PACK),
+                in_=x_scale.rearrange("o (g p t) -> p (o g) t", p=P, t=PACK),
+            )
+
+        def load_x(first, count):
+            raw = sb("x_raw_%d" % first, count * D, U8)
+            lo = (first % 2) * D
+            nc.sync.dma_start(out=raw[:], in_=x_rows[first // 2][:, lo : lo + count * D])
+            for i in range(count):
+                x_raw[first + i] = raw[:, i * D : (i + 1) * D].bitcast(FP8)
+
+        def load_words(w, g=None):
+            if g is None:
+                passes = hbm_words[w].shape[0]
+                nc.sync.dma_start(
+                    out=words[w][:].bitcast(I32).rearrange("p (g n) -> p g n", g=passes),
+                    in_=hbm_words[w].bitcast(I32).rearrange("g p n -> p g n"),
+                )
+            else:
+                nc.sync.dma_start(out=w0_pass[g][:].bitcast(I32), in_=hbm_words[w][g].bitcast(I32))
+
+        def load_scales(w, queue="Q"):
+            passes = hbm_scales[w].shape[0]
+            eng = nc.sync if queue == "Q" else nc.gpsimd
+            for quad in range(4):
+                eng.dma_start(
+                    out=scales[w][32 * quad : 32 * quad + 4, :].bitcast(I32).rearrange("p (g n) -> p g n", g=passes),
+                    in_=hbm_scales[w][:, 4 * quad : 4 * quad + 4, :].bitcast(I32).rearrange("g j n -> j g n"),
+                )
+
+        def load_gain():
+            nc.gpsimd.dma_start(
+                out=gain_rows[:].rearrange("t (q i) -> t q i", i=8),
+                in_=d.rearrange("(q t i) -> t q i", t=PACK, i=8),
+            )
+
+        def widen_gain():
+            nc.gpsimd.tensor_copy(out=gain_square[0:PACK, :], in_=gain_rows[:])
+
+        def turn_gain():
+            bank = new_bank("gain")
+            nc.tensor.transpose(bank[:, 0:P], gain_square[:], ident[:])
+
+        def empty_gain():
+            nc.scalar.copy(out=gain[:], in_=banks["gain",][:, 0:PACK])
+
+        def regroup(w):
+            for src, dst, run in ((words[w], sliced_words[w], 4), (scales[w], sliced_scales[w], 2)):
+                nc.vector.tensor_copy(
+                    out=dst[:].bitcast(I32).rearrange("p (g t q i) -> p g t q i", t=PACK, q=16, i=run),
+                    in_=src[:].bitcast(I32).rearrange("p (g q t i) -> p g t q i", t=PACK, q=16, i=run),
+                )
+
+        def spread_mm(g):
+            bank = new_bank("spread", g)
+            for t in range(PACK):
+                col = g * PACK + t
+                nc.tensor.transpose(
+                    bank[:, t * P : (t + 1) * P], x_scale_cols[:, col : col + 1].to_broadcast([P, P]), ident[:]
+                )
+
+        def spread_out(g, copy):
+            copy(
+                out=x_scale_spread[:, g * BANK : (g + 1) * BANK].rearrange("p (n t) -> p n t", t=PACK),
+                in_=banks["spread", g][:].rearrange("p (t n) -> p n t", t=PACK),
+            )
+
+        def widen_x(j, copy):
+            copy(out=x_wide[j][:], in_=x_raw[j])
+
+        def scale_x(j):
+            nc.vector.tensor_tensor(out=x_wide[j][:], in0=x_raw[j], in1=x_scale_spread[:], op=ALU.mult)
+
+        def turn_x(j):
+            bank = new_bank("x", j)
+            pairs = x_wide[j][:].bitcast(F32)
+            for g in range(PASSES):
+                for u in range(2):
+                    lo = (2 * g + u) * P
+                    nc.tensor.transpose(bank[:, lo : lo + P], pairs[:, 256 * g + u : 256 * (g + 1) : 2], ident[:])
+
+        def empty_x(j):
+            nc.scalar.copy(
+                out=x_turned[j][:].bitcast(F32).rearrange("p (g n u) -> p g n u", g=PASSES, u=2),
+                in_=banks["x", j][:].rearrange("p (g u n) -> p g n u", g=PASSES, u=2),
+            )
+
+        def scale_turned(j, g):
+            cols = slice(g * BANK, (g + 1) * BANK)
+            nc.vector.tensor_tensor(
+                out=x_turned[j][:, cols].rearrange("p (n u e) -> p n u e", u=2, e=2),
+                in0=banks["x", j][:].bitcast(BF16)[:, cols].rearrange("p (u n e) -> p n u e", u=2, e=2),
+                in1=x_scale_cols[:, g * PACK : (g + 1) * PACK]
+                .rearrange("p (u e) -> p u e", u=2)
+                .unsqueeze(1)
+                .to_broadcast([P, P, 2, 2]),
+                op=ALU.mult,
+            )
+
+        def quant_x(j, g):
+            cols = slice((j % 4) * P, (j % 4 + 1) * P)
+            nc.vector.quantize_mx(
+                out=x_codes[j // 4, g][:, cols].bitcast(FP8X4),
+                scales=x_scales[j // 4, g][:, cols],
+                in_=x_turned[j][:, g * BANK : (g + 1) * BANK],
+            )
+
+        def base_mm(j, h):
+            bank = new_bank("base", j, h)
+            cols = slice((j % 4) * P, (j % 4 + 1) * P)
+            for g in range(PASSES):
+                nc.tensor.matmul_mx(
+                    out=bank[:],
+                    lhsT=x_codes[j // 4, g][:, cols].bitcast(FP8X4),
+                    lhsT_scale=x_scales[j // 4, g][:, cols],
+                    rhs=w0_pass[g][:, 2 * h * BANK : 2 * (h + 1) * BANK].bitcast(FP4X4),
+                    rhs_scale=scales["w0"][:, g * F + h * BANK : g * F + (h + 1) * BANK],
+                    start=(g == 0),
+                    stop=(g == PASSES - 1),
+                )
+
+        def base_out(j, h):
+            nc.scalar.copy(out=result[j, h][:], in_=banks["base", j, h][:])
+
+        def down_mm(c, t):
+            bank = new_bank("down", c, t)
+            for g in range(PASSES):
+                lo = g * R + t * P
+                nc.tensor.matmul_mx(
+                    out=bank[:],
+                    lhsT=sliced_words["a"][:, 2 * lo : 2 * (lo + P)].bitcast(FP4X4),
+                    lhsT_scale=sliced_scales["a"][:, lo : lo + P],
+                    rhs=x_codes[c, g][:].bitcast(FP8X4),
+                    rhs_scale=x_scales[c, g][:],
+                    start=(g == 0),
+                    stop=(g == PASSES - 1),
+                )
+
+        def down_out(c, t):
+            nc.scalar.activation(
+                out=pg_planes[c][:, t * BANK : (t + 1) * BANK],
+                in_=banks["down", c, t][:],
+                func=ACT.Copy,
+                scale=gain[:, t : t + 1],
+            )
+
+        def weave(planes, woven, s, copy):
+            copy(
+                out=woven[:, s * 1024 : (s + 1) * 1024].rearrange("p (n i t) -> p n t i", i=4, t=PACK),
+                in_=planes[:]
+                .rearrange("p (t n) -> p t n", t=PACK)[:, :, s * 256 : (s + 1) * 256]
+                .rearrange("p t (n i) -> p n t i", i=4),
+            )
+
+        def weave_p(c, s):
+            weave(pg_planes[c], pg_woven[c], s, on_vector)
+
+        def quant_p(c, s):
+            nc.vector.quantize_mx(
+                out=pg_codes[c][:, s * 256 : (s + 1) * 256].bitcast(FP8X4),
+                scales=pg_scales[c][:, s * 256 : (s + 1) * 256],
+                in_=pg_woven[c][:, s * 1024 : (s + 1) * 1024],
+            )
+
+        def mix_mm(h, t):
+            bank = new_bank("mix", h, t)
+            nc.tensor.matmul_mx(
+                out=bank[:],
+                lhsT=sliced_words["m"][:, 2 * t * P : 2 * (t + 1) * P].bitcast(FP4X4),
+                lhsT_scale=sliced_scales["m"][:, t * P : (t + 1) * P],
+                rhs=words["bu"][:, 2 * h * BANK : 2 * (h + 1) * BANK].bitcast(FP4X4),
+                rhs_scale=scales["bu"][:, h * BANK : (h + 1) * BANK],
+                start=True,
+                stop=True,
+            )
+
+        def mix_out(h, t):
+            nc.scalar.copy(out=c_planes[h][:, t * BANK : (t + 1) * BANK], in_=banks["mix", h, t][:])
+
+        def weave_c(h, s, copy):
+            weave(c_planes[h], c_woven[h], s, copy)
+
+        def quant_c(h):
+            nc.vector.quantize_mx(out=c_codes[h][:].bitcast(FP8X4), scales=c_scales[h][:], in_=c_woven[h][:])
+
+        def up_mm(j, h):
+            bank = new_bank("up", j, h)
+            cols = slice((j % 4) * P, (j % 4 + 1) * P)
+            nc.tensor.matmul_mx(
+                out=bank[:],
+                lhsT=pg_codes[j // 4][:, cols].bitcast(FP8X4),
+                lhsT_scale=pg_scales[j // 4][:, cols],
+                rhs=c_codes[h][:].bitcast(FP8X4),
+                rhs_scale=c_scales[h][:],
+                start=True,
+                stop=True,
+            )
+
+        def finish(j, h):
+            nc.vector.scalar_tensor_tensor(
+                out=result[j, h][:],
+                in0=banks["up", j, h][:],
+                scalar=1.0 / math.sqrt(R),
+                in1=result[j, h][:],
+                op0=ALU.mult,
+                op1=ALU.add,
+            )
+
+        def store(j, h):
+            nc.sync.dma_start(out=out_rows[j // 2][j % 2][:, h * BANK : (h + 1) * BANK], in_=result[j, h][:])
+
+        for w in ("m","bu","w0","a"):
+            clear_scales(w)
+        setup()
+        load_gain()
+        load_x_scale()
+        load_x(0,1)
+        load_x(1,1)
+        load_words("m")
+        load_scales("m")
+        load_words("bu")
+        load_scales("bu")
+        load_x(2,2)
+        load_scales("a","G")
+        load_words("w0",0)
+        load_words("w0",1)
+        load_scales("w0")
+        load_x(4,2)
+        load_words("a")
+        load_x(6,2)
+        widen_x(0,on_vector)
+        widen_x(1,on_scalar_act)
+        spread_mm(0)
+        turn_x(0)
+        turn_x(1)
+        spread_mm(1)
+        widen_gain()
+        regroup("m")
+        scale_turned(0,0)
+        scale_turned(0,1)
+        spread_out(0,on_scalar)
+        spread_out(1,on_scalar)
+        scale_turned(1,0)
+        quant_x(0,0)
+        quant_x(0,1)
+        scale_turned(1,1)
+        for t in range(4):
+            mix_mm(0,t)
+            mix_out(0,t)
+        scale_x(2)
+        quant_x(1,0)
+        quant_x(1,1)
+        scale_x(3)
+        mix_mm(1,0)
+        mix_mm(1,1)
+        base_mm(0,0)
+        turn_x(2)
+        empty_x(2)
+        mix_out(1,0)
+        mix_mm(1,2)
+        mix_mm(1,3)
+        turn_x(3)
+        turn_gain()
+        empty_x(3)
+        empty_gain()
+        mix_out(1,1)
+        scale_x(4)
+        regroup("a")
+        quant_x(2,0)
+        quant_x(2,1)
+        scale_x(5)
+        quant_x(3,0)
+        quant_x(3,1)
+        scale_x(6)
+        base_mm(1,0)
+        turn_x(4)
+        mix_out(1,2)
+        empty_x(4)
+        base_mm(2,0)
+        turn_x(5)
+        mix_out(1,3)
+        empty_x(5)
+        down_mm(0,0)
+        down_mm(0,1)
+        down_out(0,0)
+        down_out(0,1)
+        scale_x(7)
+        quant_x(4,0)
+        quant_x(4,1)
+        quant_x(5,0)
+        quant_x(5,1)
+        weave_c(0,0,on_vector)
+        turn_x(6)
+        turn_x(7)
+        empty_x(6)
+        empty_x(7)
+        down_mm(0,2)
+        down_mm(0,3)
+        down_out(0,2)
+        down_out(0,3)
+        weave_c(0,1,on_vector)
+        quant_x(6,0)
+        quant_x(6,1)
+        quant_x(7,0)
+        quant_x(7,1)
+        quant_c(0)
+        base_mm(3,0)
+        base_mm(0,1)
+        base_out(0,0)
+        base_out(1,0)
+        weave_p(0,0)
+        weave_p(0,1)
+        quant_p(0,0)
+        weave_c(1,0,on_vector)
+        quant_p(0,1)
+        for t in range(4):
+            down_mm(1,t)
+            down_out(1,t)
+        base_out(2,0)
+        base_out(3,0)
+        weave_c(1,1,on_scalar)
+        base_out(0,1)
+        up_mm(0,0)
+        up_mm(1,0)
+        up_mm(2,0)
+        up_mm(3,0)
+        finish(0,0)
+        store(0,0)
+        finish(1,0)
+        store(1,0)
+        base_mm(4,0)
+        base_mm(5,0)
+        base_out(4,0)
+        base_out(5,0)
+        weave_p(1,0)
+        finish(2,0)
+        store(2,0)
+        quant_p(1,0)
+        finish(3,0)
+        store(3,0)
+        weave_p(1,1)
+        quant_c(1)
+        quant_p(1,1)
+        base_mm(6,0)
+        base_mm(7,0)
+        base_out(6,0)
+        base_out(7,0)
+        up_mm(4,0)
+        up_mm(5,0)
+        base_mm(1,1)
+        base_mm(2,1)
+        finish(4,0)
+        store(4,0)
+        finish(5,0)
+        store(5,0)
+        base_out(1,1)
+        base_out(2,1)
+        up_mm(6,0)
+        up_mm(7,0)
+        base_mm(3,1)
+        base_mm(4,1)
+        finish(6,0)
+        store(6,0)
+        finish(7,0)
+        store(7,0)
+        base_out(3,1)
+        base_out(4,1)
+        up_mm(0,1)
+        up_mm(1,1)
+        base_mm(5,1)
+        base_mm(6,1)
+        finish(0,1)
+        store(0,1)
+        finish(1,1)
+        store(1,1)
+        base_out(5,1)
+        base_out(6,1)
+        up_mm(2,1)
+        up_mm(3,1)
+        base_mm(7,1)
+        finish(2,1)
+        store(2,1)
+        finish(3,1)
+        store(3,1)
+        base_out(7,1)
+        for j in range(4,8):
+            up_mm(j,1)
+            finish(j,1)
+            store(j,1)

@@ -56,7 +56,9 @@ def tile_moslorasubspacemixerrankgain_w4_kernel(
         out_rows = out.rearrange("(h p j) f -> h j p f", p=P, j=2)
         x_raw = {}
         x_wide = [sb("x_wide_%d" % j, D, BF16) for j in range(TILES)]
-        x_turned = [sb("x_turned_%d" % j, D, BF16) for j in range(TILES)]
+        x_turned = [sb("x_turned_%d" % i, 2 * D, BF16) for i in range(TILES // 2)]
+        first_wide = [sb("first_wide_%d" % g, BANK, BF16) for g in range(PASSES)]
+        warm_operand = sb("warm_operand", BANK, BF16)
         x_codes = {(c, g): sb("x_codes_%d_%d" % (c, g), BANK, U32) for c in range(2) for g in range(PASSES)}
         x_scales = {(c, g): sb("x_scales_%d_%d" % (c, g), BANK, U8) for c in range(2) for g in range(PASSES)}
         pg_planes = [sb("pg_planes_%d" % c, PACK * BANK, BF16) for c in range(2)]
@@ -110,10 +112,10 @@ def tile_moslorasubspacemixerrankgain_w4_kernel(
             else:
                 nc.sync.dma_start(out=w0_pass[g][:].bitcast(I32), in_=hbm_words[w][g].bitcast(I32))
 
-        def load_scales(w, queue="Q"):
+        def load_scales(w, queue="Q", quads=range(4)):
             passes = hbm_scales[w].shape[0]
             eng = nc.sync if queue == "Q" else nc.gpsimd
-            for quad in range(4):
+            for quad in quads:
                 eng.dma_start(
                     out=scales[w][32 * quad : 32 * quad + 4, :].bitcast(I32).rearrange("p (g n) -> p g n", g=passes),
                     in_=hbm_scales[w][:, 4 * quad : 4 * quad + 4, :].bitcast(I32).rearrange("g j n -> j g n"),
@@ -172,15 +174,15 @@ def tile_moslorasubspacemixerrankgain_w4_kernel(
 
         def empty_x(j):
             nc.scalar.copy(
-                out=x_turned[j][:].bitcast(F32).rearrange("p (g n u) -> p g n u", g=PASSES, u=2),
+                out=x_turned[j // 2][:].bitcast(F32).rearrange("p (g j n u) -> p g j n u", g=PASSES, j=2, u=2)[:, :, j % 2],
                 in_=banks["x", j][:].rearrange("p (g u n) -> p g n u", g=PASSES, u=2),
             )
 
-        def scale_turned(j, g):
-            cols = slice(g * BANK, (g + 1) * BANK)
+        def scale_pass(j, g, turned):
+            lo = (2 * g + j % 2) * BANK
             nc.vector.tensor_tensor(
-                out=x_turned[j][:, cols].rearrange("p (n u e) -> p n u e", u=2, e=2),
-                in0=banks["x", j][:].bitcast(BF16)[:, cols].rearrange("p (u n e) -> p n u e", u=2, e=2),
+                out=x_turned[j // 2][:, lo : lo + BANK].rearrange("p (n u e) -> p n u e", u=2, e=2),
+                in0=turned.rearrange("p (u n e) -> p n u e", u=2, e=2),
                 in1=x_scale_cols[:, g * PACK : (g + 1) * PACK]
                 .rearrange("p (u e) -> p u e", u=2)
                 .unsqueeze(1)
@@ -188,12 +190,35 @@ def tile_moslorasubspacemixerrankgain_w4_kernel(
                 op=ALU.mult,
             )
 
-        def quant_x(j, g):
-            cols = slice((j % 4) * P, (j % 4 + 1) * P)
+        def scale_turned(j, g):
+            scale_pass(j, g, banks["x", j][:].bitcast(BF16)[:, g * BANK : (g + 1) * BANK])
+
+        def warm_tile():
+            nc.vector.memset(warm_operand[:].bitcast(I32), 0)
+
+        def warm(count):
+            bank = new_bank("warm")
+            for i in range(count):
+                nc.tensor.matmul(bank[:], lhsT=warm_operand[:, 0:P], rhs=warm_operand[:], start=True, stop=True)
+
+        def widen_first(g):
+            nc.vector.tensor_copy(out=first_wide[g][:], in_=x_raw[0][:, g * BANK : (g + 1) * BANK])
+
+        def turn_first(g):
+            bank = new_bank("first", g)
+            pairs = first_wide[g][:].bitcast(F32)
+            for u in range(2):
+                nc.tensor.transpose(bank[:, u * P : (u + 1) * P], pairs[:, u:256:2], ident[:])
+
+        def scale_first(g):
+            scale_pass(0, g, banks["first", g][:].bitcast(BF16)[:, 0:BANK])
+
+        def quant_x(first, count, g):
+            cols = slice((first % 4) * P, (first % 4 + count) * P)
             nc.vector.quantize_mx(
-                out=x_codes[j // 4, g][:, cols].bitcast(FP8X4),
-                scales=x_scales[j // 4, g][:, cols],
-                in_=x_turned[j][:, g * BANK : (g + 1) * BANK],
+                out=x_codes[first // 4, g][:, cols].bitcast(FP8X4),
+                scales=x_scales[first // 4, g][:, cols],
+                in_=x_turned[first // 2][:, (2 * g + first % 2) * BANK : (2 * g + first % 2 + count) * BANK],
             )
 
         def base_mm(j, h):
@@ -287,31 +312,35 @@ def tile_moslorasubspacemixerrankgain_w4_kernel(
                 stop=True,
             )
 
-        def finish(j, h):
+        def finish(j, h, lo=0, hi=BANK):
             nc.vector.scalar_tensor_tensor(
-                out=result[j, h][:],
-                in0=banks["up", j, h][:],
+                out=result[j, h][:, lo:hi],
+                in0=banks["up", j, h][:, lo:hi],
                 scalar=1.0 / math.sqrt(R),
-                in1=result[j, h][:],
+                in1=result[j, h][:, lo:hi],
                 op0=ALU.mult,
                 op1=ALU.add,
             )
 
-        def store(j, h):
-            nc.sync.dma_start(out=out_rows[j // 2][j % 2][:, h * BANK : (h + 1) * BANK], in_=result[j, h][:])
+        def store(j, h, lo=0, hi=BANK):
+            nc.sync.dma_start(
+                out=out_rows[j // 2][j % 2][:, h * BANK + lo : h * BANK + hi], in_=result[j, h][:, lo:hi]
+            )
 
+        warm_tile()
         for w in ("m","bu","w0","a"):
             clear_scales(w)
         setup()
-        load_gain()
-        load_x_scale()
         load_x(0,1)
+        load_x_scale()
         load_x(1,1)
         load_words("m")
-        load_scales("m")
         load_words("bu")
-        load_scales("bu")
+        load_scales("m")
+        load_scales("bu","G",(0,1))
+        load_scales("bu","Q",(2,3))
         load_x(2,2)
+        load_gain()
         load_scales("a","G")
         load_words("w0",0)
         load_words("w0",1)
@@ -319,162 +348,168 @@ def tile_moslorasubspacemixerrankgain_w4_kernel(
         load_x(4,2)
         load_words("a")
         load_x(6,2)
-        widen_x(0,on_vector)
+        warm(3)
+        widen_first(0)
+        widen_first(1)
         widen_x(1,on_scalar_act)
+        turn_first(0)
+        turn_first(1)
         spread_mm(0)
-        turn_x(0)
-        turn_x(1)
         spread_mm(1)
+        turn_x(1)
+        warm(1)
         widen_gain()
+        scale_first(0)
+        scale_first(1)
         regroup("m")
-        scale_turned(0,0)
-        scale_turned(0,1)
         spread_out(0,on_scalar)
         spread_out(1,on_scalar)
         scale_turned(1,0)
-        quant_x(0,0)
-        quant_x(0,1)
+        quant_x(0,1,0)
+        quant_x(0,1,1)
         scale_turned(1,1)
         for t in range(4):
             mix_mm(0,t)
             mix_out(0,t)
         scale_x(2)
-        quant_x(1,0)
-        quant_x(1,1)
+        quant_x(1,1,0)
+        quant_x(1,1,1)
         scale_x(3)
-        mix_mm(1,0)
-        mix_mm(1,1)
+        for t in range(4):
+            mix_mm(1,t)
         base_mm(0,0)
-        turn_x(2)
-        empty_x(2)
         mix_out(1,0)
-        mix_mm(1,2)
-        mix_mm(1,3)
+        mix_out(1,1)
+        base_mm(0,1)
+        turn_x(2)
         turn_x(3)
         turn_gain()
+        empty_x(2)
         empty_x(3)
         empty_gain()
-        mix_out(1,1)
         scale_x(4)
         regroup("a")
-        quant_x(2,0)
-        quant_x(2,1)
         scale_x(5)
-        quant_x(3,0)
-        quant_x(3,1)
+        quant_x(2,2,0)
+        quant_x(2,2,1)
         scale_x(6)
         base_mm(1,0)
-        turn_x(4)
         mix_out(1,2)
-        empty_x(4)
-        base_mm(2,0)
-        turn_x(5)
         mix_out(1,3)
+        base_mm(1,1)
+        turn_x(4)
+        turn_x(5)
+        base_out(0,0)
+        empty_x(4)
         empty_x(5)
         down_mm(0,0)
         down_mm(0,1)
         down_out(0,0)
         down_out(0,1)
         scale_x(7)
-        quant_x(4,0)
-        quant_x(4,1)
-        quant_x(5,0)
-        quant_x(5,1)
         weave_c(0,0,on_vector)
+        quant_x(4,2,0)
+        quant_x(4,2,1)
+        weave_c(0,1,on_vector)
+        down_mm(0,2)
         turn_x(6)
         turn_x(7)
+        down_out(0,2)
         empty_x(6)
         empty_x(7)
-        down_mm(0,2)
         down_mm(0,3)
-        down_out(0,2)
         down_out(0,3)
-        weave_c(0,1,on_vector)
-        quant_x(6,0)
-        quant_x(6,1)
-        quant_x(7,0)
-        quant_x(7,1)
+        weave_c(1,0,on_vector)
+        quant_x(6,2,0)
+        quant_x(6,2,1)
         quant_c(0)
-        base_mm(3,0)
-        base_mm(0,1)
-        base_out(0,0)
+        base_mm(2,0)
+        base_mm(2,1)
+        base_out(0,1)
+        weave_c(1,1,on_scalar)
         base_out(1,0)
         weave_p(0,0)
         weave_p(0,1)
         quant_p(0,0)
-        weave_c(1,0,on_vector)
+        quant_c(1)
         quant_p(0,1)
+        base_mm(3,0)
         for t in range(4):
             down_mm(1,t)
             down_out(1,t)
+        base_out(1,1)
         base_out(2,0)
-        base_out(3,0)
-        weave_c(1,1,on_scalar)
-        base_out(0,1)
+        base_out(2,1)
         up_mm(0,0)
+        up_mm(0,1)
         up_mm(1,0)
-        up_mm(2,0)
-        up_mm(3,0)
         finish(0,0)
         store(0,0)
-        finish(1,0)
-        store(1,0)
-        base_mm(4,0)
-        base_mm(5,0)
-        base_out(4,0)
-        base_out(5,0)
-        weave_p(1,0)
-        finish(2,0)
-        store(2,0)
-        quant_p(1,0)
-        finish(3,0)
-        store(3,0)
-        weave_p(1,1)
-        quant_c(1)
-        quant_p(1,1)
-        base_mm(6,0)
-        base_mm(7,0)
-        base_out(6,0)
-        base_out(7,0)
-        up_mm(4,0)
-        up_mm(5,0)
-        base_mm(1,1)
-        base_mm(2,1)
-        finish(4,0)
-        store(4,0)
-        finish(5,0)
-        store(5,0)
-        base_out(1,1)
-        base_out(2,1)
-        up_mm(6,0)
-        up_mm(7,0)
-        base_mm(3,1)
-        base_mm(4,1)
-        finish(6,0)
-        store(6,0)
-        finish(7,0)
-        store(7,0)
-        base_out(3,1)
-        base_out(4,1)
-        up_mm(0,1)
-        up_mm(1,1)
-        base_mm(5,1)
-        base_mm(6,1)
         finish(0,1)
         store(0,1)
+        base_mm(3,1)
+        up_mm(1,1)
+        base_out(3,0)
+        base_out(3,1)
+        weave_p(1,0)
+        finish(1,0)
+        store(1,0)
+        weave_p(1,1)
         finish(1,1)
         store(1,1)
-        base_out(5,1)
-        base_out(6,1)
+        quant_p(1,0)
+        up_mm(2,0)
         up_mm(2,1)
-        up_mm(3,1)
-        base_mm(7,1)
+        base_mm(4,0)
+        base_mm(4,1)
+        base_out(4,0)
+        base_out(4,1)
+        finish(2,0)
+        store(2,0)
+        quant_p(1,1)
         finish(2,1)
         store(2,1)
+        up_mm(3,0)
+        up_mm(3,1)
+        base_mm(5,0)
+        base_mm(5,1)
+        base_out(5,0)
+        base_out(5,1)
+        finish(3,0)
+        store(3,0)
         finish(3,1)
         store(3,1)
+        up_mm(4,0)
+        up_mm(4,1)
+        base_mm(6,0)
+        base_mm(6,1)
+        base_out(6,0)
+        base_out(6,1)
+        finish(4,0)
+        store(4,0)
+        finish(4,1)
+        store(4,1)
+        up_mm(5,0)
+        up_mm(5,1)
+        base_mm(7,0)
+        up_mm(6,0)
+        base_mm(7,1)
+        base_out(7,0)
         base_out(7,1)
-        for j in range(4,8):
-            up_mm(j,1)
-            finish(j,1)
-            store(j,1)
+        finish(5,0)
+        store(5,0)
+        finish(5,1)
+        store(5,1)
+        up_mm(6,1)
+        up_mm(7,0)
+        up_mm(7,1)
+        finish(6,0)
+        store(6,0)
+        finish(6,1)
+        store(6,1)
+        finish(7,0)
+        store(7,0)
+        finish(7,1,0,256)
+        store(7,1,0,256)
+        finish(7,1,256,512)
+        store(7,1,256,512)

@@ -40,8 +40,7 @@ def tile_moslorasubspacemixerrankgain_w4_kernel(
         hbm_words = {"w0": w0_words, "a": a_words, "m": m_words, "bu": bu_words}
         hbm_scales = {"w0": w0_scales, "a": a_scales, "m": m_scales, "bu": bu_scales}
         scales = {w: sb(w + "_scale_rows", s.shape[0] * s.shape[2], U8) for w, s in hbm_scales.items()}
-        words = {w: sb(w + "_code_words", hbm_words[w].shape[0] * hbm_words[w].shape[2], U8) for w in ("a", "m", "bu")}
-        w0_pass = [sb("w0_code_words_%d" % g, 2 * F, U8) for g in range(PASSES)]
+        words = {w: sb(w + "_code_words", hbm_words[w].shape[0] * hbm_words[w].shape[2], U8) for w in hbm_words}
         sliced_words = {w: sb(w + "_sliced_words", words[w].shape[1], U8) for w in ("a", "m")}
         sliced_scales = {w: sb(w + "_sliced_scales", scales[w].shape[1], U8) for w in ("a", "m")}
 
@@ -82,8 +81,8 @@ def tile_moslorasubspacemixerrankgain_w4_kernel(
         def on_scalar_act(out, in_):
             nc.scalar.activation(out=out, in_=in_, func=ACT.Copy)
 
-        def clear_scales(w):
-            nc.vector.memset(scales[w][:].bitcast(I32), 0)
+        def clear_scales(w, engine):
+            engine.memset(scales[w][:].bitcast(I32), 0)
 
         def setup():
             make_identity(nc, ident[:])
@@ -97,38 +96,40 @@ def tile_moslorasubspacemixerrankgain_w4_kernel(
 
         def load_x(first, count):
             raw = sb("x_raw_%d" % first, count * D, U8)
-            lo = (first % 2) * D
-            nc.sync.dma_start(out=raw[:], in_=x_rows[first // 2][:, lo : lo + count * D])
+            if count == 1:
+                lo = (first % 2) * D
+                nc.sync.dma_start(out=raw[:], in_=x_rows[first // 2][:, lo : lo + D])
+            else:
+                nc.sync.dma_start(
+                    out=raw[:].rearrange("p (h c) -> p h c", c=2 * D),
+                    in_=x_rows[first // 2 : (first + count) // 2].rearrange("h p c -> p h c"),
+                )
             for i in range(count):
                 x_raw[first + i] = raw[:, i * D : (i + 1) * D].bitcast(FP8)
 
-        def load_words(w, g=None):
-            if g is None:
-                passes = hbm_words[w].shape[0]
-                nc.sync.dma_start(
-                    out=words[w][:].bitcast(I32).rearrange("p (g n) -> p g n", g=passes),
-                    in_=hbm_words[w].bitcast(I32).rearrange("g p n -> p g n"),
-                )
-            else:
-                nc.sync.dma_start(out=w0_pass[g][:].bitcast(I32), in_=hbm_words[w][g].bitcast(I32))
+        def load_words(w):
+            passes = hbm_words[w].shape[0]
+            nc.sync.dma_start(
+                out=words[w][:].bitcast(I32).rearrange("p (g n) -> p g n", g=passes),
+                in_=hbm_words[w].bitcast(I32).rearrange("g p n -> p g n"),
+            )
 
-        def load_scales(w, queue="Q", quads=range(4)):
+        def load_scales(w, quads=range(4)):
             passes = hbm_scales[w].shape[0]
-            eng = nc.sync if queue == "Q" else nc.gpsimd
             for quad in quads:
-                eng.dma_start(
+                nc.sync.dma_start(
                     out=scales[w][32 * quad : 32 * quad + 4, :].bitcast(I32).rearrange("p (g n) -> p g n", g=passes),
                     in_=hbm_scales[w][:, 4 * quad : 4 * quad + 4, :].bitcast(I32).rearrange("g j n -> j g n"),
                 )
 
         def load_gain():
-            nc.gpsimd.dma_start(
+            nc.sync.dma_start(
                 out=gain_rows[:].rearrange("t (q i) -> t q i", i=8),
                 in_=d.rearrange("(q t i) -> t q i", t=PACK, i=8),
             )
 
         def widen_gain():
-            nc.gpsimd.tensor_copy(out=gain_square[0:PACK, :], in_=gain_rows[:])
+            nc.scalar.copy(out=gain_square[0:PACK, :], in_=gain_rows[:])
 
         def turn_gain():
             bank = new_bank("gain")
@@ -229,7 +230,7 @@ def tile_moslorasubspacemixerrankgain_w4_kernel(
                     out=bank[:],
                     lhsT=x_codes[j // 4, g][:, cols].bitcast(FP8X4),
                     lhsT_scale=x_scales[j // 4, g][:, cols],
-                    rhs=w0_pass[g][:, 2 * h * BANK : 2 * (h + 1) * BANK].bitcast(FP4X4),
+                    rhs=words["w0"][:, 2 * (g * F + h * BANK) : 2 * (g * F + (h + 1) * BANK)].bitcast(FP4X4),
                     rhs_scale=scales["w0"][:, g * F + h * BANK : g * F + (h + 1) * BANK],
                     start=(g == 0),
                     stop=(g == PASSES - 1),
@@ -327,27 +328,26 @@ def tile_moslorasubspacemixerrankgain_w4_kernel(
                 out=out_rows[j // 2][j % 2][:, h * BANK + lo : h * BANK + hi], in_=result[j, h][:, lo:hi]
             )
 
+        clear_scales("m",nc.gpsimd)
+        clear_scales("bu",nc.gpsimd)
         warm_tile()
-        for w in ("m","bu","w0","a"):
-            clear_scales(w)
+        clear_scales("w0",nc.vector)
+        clear_scales("a",nc.vector)
         setup()
         load_x(0,1)
         load_x_scale()
         load_x(1,1)
         load_words("m")
-        load_words("bu")
         load_scales("m")
-        load_scales("bu","G",(0,1))
-        load_scales("bu","Q",(2,3))
+        load_words("bu")
+        load_scales("bu")
         load_x(2,2)
+        load_words("w0")
         load_gain()
-        load_scales("a","G")
-        load_words("w0",0)
-        load_words("w0",1)
         load_scales("w0")
-        load_x(4,2)
+        load_x(4,4)
         load_words("a")
-        load_x(6,2)
+        load_scales("a")
         warm(3)
         widen_first(0)
         widen_first(1)
@@ -358,12 +358,12 @@ def tile_moslorasubspacemixerrankgain_w4_kernel(
         spread_mm(1)
         turn_x(1)
         warm(1)
-        widen_gain()
         scale_first(0)
         scale_first(1)
         regroup("m")
         spread_out(0,on_scalar)
         spread_out(1,on_scalar)
+        widen_gain()
         scale_turned(1,0)
         quant_x(0,1,0)
         quant_x(0,1,1)

@@ -19,10 +19,17 @@ ALU = mybir.AluOpType
 ACT = mybir.ActivationFunctionType
 
 P = 128
-PACK = 4
+SLOTS = 4
 BANK = 512
+PSUM_BANKS = 8
 TILES = N // P
 PASSES = D // BANK
+CHUNKS = N // BANK
+TILES_A_CHUNK = TILES // CHUNKS
+HALVES = F // BANK
+QUADRANTS = 4
+GROUPS = 16
+PIECE = 256
 
 
 def tile_moslorasubspacemixerrankgain_w4_kernel(
@@ -31,7 +38,7 @@ def tile_moslorasubspacemixerrankgain_w4_kernel(
     nc = tc.nc
     with ExitStack() as ctx:
         keep = ctx.enter_context(tc.tile_pool(name="keep", bufs=1))
-        psum = ctx.enter_context(tc.psum_pool(name="psum", bufs=8))
+        psum = ctx.enter_context(tc.psum_pool(name="psum", bufs=PSUM_BANKS))
         ctx.enter_context(tc.manual_schedule())
 
         def sb(name, cols, dtype, rows=P):
@@ -40,58 +47,51 @@ def tile_moslorasubspacemixerrankgain_w4_kernel(
         hbm_words = {"w0": w0_words, "a": a_words, "m": m_words, "bu": bu_words}
         hbm_scales = {"w0": w0_scales, "a": a_scales, "m": m_scales, "bu": bu_scales}
         scales = {w: sb(w + "_scale_rows", s.shape[0] * s.shape[2], U8) for w, s in hbm_scales.items()}
-        words = {w: sb(w + "_code_words", hbm_words[w].shape[0] * hbm_words[w].shape[2], U8) for w in hbm_words}
+        words = {w: sb(w + "_code_words", s.shape[0] * s.shape[2], U8) for w, s in hbm_words.items()}
         sliced_words = {w: sb(w + "_sliced_words", words[w].shape[1], U8) for w in ("a", "m")}
         sliced_scales = {w: sb(w + "_sliced_scales", scales[w].shape[1], U8) for w in ("a", "m")}
 
         ident = sb("ident", P, F32)
-        gain_rows = sb("gain_rows", P, BF16, rows=PACK)
+        gain_rows = sb("gain_rows", P, BF16, rows=SLOTS)
         gain_square = sb("gain_square", P, F32)
-        gain = sb("gain", PACK, F32)
-        x_scale_cols = sb("x_scale_cols", PASSES * PACK, F32)
+        gain = sb("gain", SLOTS, F32)
+        x_scale_cols = sb("x_scale_cols", PASSES * SLOTS, F32)
         x_scale_spread = sb("x_scale_spread", D, F32)
 
-        x_rows = x_bytes.rearrange("(h p j) k -> h p (j k)", p=P, j=2)
-        out_rows = out.rearrange("(h p j) f -> h j p f", p=P, j=2)
+        x_rows = x_bytes.rearrange("(h n e) k -> h n (e k)", n=P, e=2)
+        out_rows = out.rearrange("(h n e) f -> h e n f", n=P, e=2)
         x_raw = {}
-        x_wide = [sb("x_wide_%d" % j, D, BF16) for j in range(TILES)]
+        x_wide = {j: sb("x_wide_%d" % j, D, BF16) for j in range(1, TILES)}
         x_turned = [sb("x_turned_%d" % i, 2 * D, BF16) for i in range(TILES // 2)]
         first_wide = [sb("first_wide_%d" % g, BANK, BF16) for g in range(PASSES)]
         warm_operand = sb("warm_operand", BANK, BF16)
-        x_codes = {(c, g): sb("x_codes_%d_%d" % (c, g), BANK, U32) for c in range(2) for g in range(PASSES)}
-        x_scales = {(c, g): sb("x_scales_%d_%d" % (c, g), BANK, U8) for c in range(2) for g in range(PASSES)}
-        pg_planes = [sb("pg_planes_%d" % c, PACK * BANK, BF16) for c in range(2)]
-        pg_woven = [sb("pg_woven_%d" % c, PACK * BANK, BF16) for c in range(2)]
-        pg_codes = [sb("pg_codes_%d" % c, BANK, U32) for c in range(2)]
-        pg_scales = [sb("pg_scales_%d" % c, BANK, U8) for c in range(2)]
-        c_planes = [sb("c_planes_%d" % h, PACK * BANK, BF16) for h in range(2)]
-        c_woven = [sb("c_woven_%d" % h, PACK * BANK, BF16) for h in range(2)]
-        c_codes = [sb("c_codes_%d" % h, BANK, U32) for h in range(2)]
-        c_scales = [sb("c_scales_%d" % h, BANK, U8) for h in range(2)]
-        result = {(j, h): sb("result_%d_%d" % (j, h), BANK, F32) for j in range(TILES) for h in range(2)}
+        x_codes = {(c, g): sb("x_codes_%d_%d" % (c, g), BANK, U32) for c in range(CHUNKS) for g in range(PASSES)}
+        x_scales = {(c, g): sb("x_scales_%d_%d" % (c, g), BANK, U8) for c in range(CHUNKS) for g in range(PASSES)}
+        pg_planes = [sb("pg_planes_%d" % c, SLOTS * BANK, BF16) for c in range(CHUNKS)]
+        pg_woven = [sb("pg_woven_%d" % c, SLOTS * BANK, BF16) for c in range(CHUNKS)]
+        pg_codes = [sb("pg_codes_%d" % c, BANK, U32) for c in range(CHUNKS)]
+        pg_scales = [sb("pg_scales_%d" % c, BANK, U8) for c in range(CHUNKS)]
+        c_planes = [sb("c_planes_%d" % h, SLOTS * BANK, BF16) for h in range(HALVES)]
+        c_woven = [sb("c_woven_%d" % h, SLOTS * BANK, BF16) for h in range(HALVES)]
+        c_codes = [sb("c_codes_%d" % h, BANK, U32) for h in range(HALVES)]
+        c_scales = [sb("c_scales_%d" % h, BANK, U8) for h in range(HALVES)]
+        result = {(j, h): sb("result_%d_%d" % (j, h), BANK, F32) for j in range(TILES) for h in range(HALVES)}
         banks = {}
 
         def new_bank(*key):
             banks[key] = psum.tile([P, BANK], F32, name="bank", tag="bank")
             return banks[key]
 
-        on_vector = nc.vector.tensor_copy
-        on_scalar = nc.scalar.copy
-
-        def on_scalar_act(out, in_):
-            nc.scalar.activation(out=out, in_=in_, func=ACT.Copy)
+        def tile_cols(j, count=1):
+            return slice((j % TILES_A_CHUNK) * P, (j % TILES_A_CHUNK + count) * P)
 
         def clear_scales(w, engine):
             engine.memset(scales[w][:].bitcast(I32), 0)
 
-        def setup():
-            make_identity(nc, ident[:])
-            nc.gpsimd.memset(gain_square[:], 0.0)
-
         def load_x_scale():
             nc.sync.dma_start(
-                out=x_scale_cols[:].rearrange("p (g t) -> p g t", t=PACK),
-                in_=x_scale.rearrange("o (g p t) -> p (o g) t", p=P, t=PACK),
+                out=x_scale_cols[:].rearrange("p (g t) -> p g t", t=SLOTS),
+                in_=x_scale.rearrange("o (g p t) -> p (o g) t", p=P, t=SLOTS),
             )
 
         def load_x(first, count):
@@ -101,8 +101,8 @@ def tile_moslorasubspacemixerrankgain_w4_kernel(
                 nc.sync.dma_start(out=raw[:], in_=x_rows[first // 2][:, lo : lo + D])
             else:
                 nc.sync.dma_start(
-                    out=raw[:].rearrange("p (h c) -> p h c", c=2 * D),
-                    in_=x_rows[first // 2 : (first + count) // 2].rearrange("h p c -> p h c"),
+                    out=raw[:].rearrange("n (h c) -> n h c", c=2 * D),
+                    in_=x_rows[first // 2 : (first + count) // 2].rearrange("h n c -> n h c"),
                 )
             for i in range(count):
                 x_raw[first + i] = raw[:, i * D : (i + 1) * D].bitcast(FP8)
@@ -114,9 +114,9 @@ def tile_moslorasubspacemixerrankgain_w4_kernel(
                 in_=hbm_words[w].bitcast(I32).rearrange("g p n -> p g n"),
             )
 
-        def load_scales(w, quads=range(4)):
+        def load_scales(w):
             passes = hbm_scales[w].shape[0]
-            for quad in quads:
+            for quad in range(QUADRANTS):
                 nc.sync.dma_start(
                     out=scales[w][32 * quad : 32 * quad + 4, :].bitcast(I32).rearrange("p (g n) -> p g n", g=passes),
                     in_=hbm_scales[w][:, 4 * quad : 4 * quad + 4, :].bitcast(I32).rearrange("g j n -> j g n"),
@@ -125,42 +125,44 @@ def tile_moslorasubspacemixerrankgain_w4_kernel(
         def load_gain():
             nc.sync.dma_start(
                 out=gain_rows[:].rearrange("t (q i) -> t q i", i=8),
-                in_=d.rearrange("(q t i) -> t q i", t=PACK, i=8),
+                in_=d.rearrange("(q t i) -> t q i", t=SLOTS, i=8),
             )
 
         def widen_gain():
-            nc.scalar.copy(out=gain_square[0:PACK, :], in_=gain_rows[:])
+            nc.scalar.copy(out=gain_square[0:SLOTS, :], in_=gain_rows[:])
 
         def turn_gain():
             bank = new_bank("gain")
             nc.tensor.transpose(bank[:, 0:P], gain_square[:], ident[:])
 
         def empty_gain():
-            nc.scalar.copy(out=gain[:], in_=banks["gain",][:, 0:PACK])
+            nc.scalar.copy(out=gain[:], in_=banks["gain",][:, 0:SLOTS])
 
         def regroup(w):
             for src, dst, run in ((words[w], sliced_words[w], 4), (scales[w], sliced_scales[w], 2)):
                 nc.vector.tensor_copy(
-                    out=dst[:].bitcast(I32).rearrange("p (g t q i) -> p g t q i", t=PACK, q=16, i=run),
-                    in_=src[:].bitcast(I32).rearrange("p (g q t i) -> p g t q i", t=PACK, q=16, i=run),
+                    out=dst[:].bitcast(I32).rearrange("p (g t q i) -> p g t q i", t=SLOTS, q=GROUPS, i=run),
+                    in_=src[:].bitcast(I32).rearrange("p (g q t i) -> p g t q i", t=SLOTS, q=GROUPS, i=run),
                 )
 
         def spread_mm(g):
             bank = new_bank("spread", g)
-            for t in range(PACK):
-                col = g * PACK + t
+            for t in range(SLOTS):
+                col = g * SLOTS + t
                 nc.tensor.transpose(
                     bank[:, t * P : (t + 1) * P], x_scale_cols[:, col : col + 1].to_broadcast([P, P]), ident[:]
                 )
 
-        def spread_out(g, copy):
-            copy(
-                out=x_scale_spread[:, g * BANK : (g + 1) * BANK].rearrange("p (n t) -> p n t", t=PACK),
-                in_=banks["spread", g][:].rearrange("p (t n) -> p n t", t=PACK),
+        def spread_out(g):
+            nc.scalar.copy(
+                out=x_scale_spread[:, g * BANK : (g + 1) * BANK].rearrange("q (p t) -> q p t", t=SLOTS),
+                in_=banks["spread", g][:].rearrange("q (t p) -> q p t", t=SLOTS),
             )
 
-        def widen_x(j, copy):
-            copy(out=x_wide[j][:], in_=x_raw[j])
+        def warm(count):
+            bank = new_bank("warm")
+            for repeat in range(count):
+                nc.tensor.matmul(bank[:], lhsT=warm_operand[:, 0:P], rhs=warm_operand[:], start=True, stop=True)
 
         def scale_x(j):
             nc.vector.tensor_tensor(out=x_wide[j][:], in0=x_raw[j], in1=x_scale_spread[:], op=ALU.mult)
@@ -168,39 +170,19 @@ def tile_moslorasubspacemixerrankgain_w4_kernel(
         def turn_x(j):
             bank = new_bank("x", j)
             pairs = x_wide[j][:].bitcast(F32)
+            half = BANK // 2
             for g in range(PASSES):
                 for u in range(2):
                     lo = (2 * g + u) * P
-                    nc.tensor.transpose(bank[:, lo : lo + P], pairs[:, 256 * g + u : 256 * (g + 1) : 2], ident[:])
+                    nc.tensor.transpose(bank[:, lo : lo + P], pairs[:, half * g + u : half * (g + 1) : 2], ident[:])
 
         def empty_x(j):
             nc.scalar.copy(
-                out=x_turned[j // 2][:].bitcast(F32).rearrange("p (g j n u) -> p g j n u", g=PASSES, j=2, u=2)[:, :, j % 2],
+                out=x_turned[j // 2][:].bitcast(F32).rearrange("p (g e n u) -> p g e n u", g=PASSES, e=2, u=2)[
+                    :, :, j % 2
+                ],
                 in_=banks["x", j][:].rearrange("p (g u n) -> p g n u", g=PASSES, u=2),
             )
-
-        def scale_pass(j, g, turned):
-            lo = (2 * g + j % 2) * BANK
-            nc.vector.tensor_tensor(
-                out=x_turned[j // 2][:, lo : lo + BANK].rearrange("p (n u e) -> p n u e", u=2, e=2),
-                in0=turned.rearrange("p (u n e) -> p n u e", u=2, e=2),
-                in1=x_scale_cols[:, g * PACK : (g + 1) * PACK]
-                .rearrange("p (u e) -> p u e", u=2)
-                .unsqueeze(1)
-                .to_broadcast([P, P, 2, 2]),
-                op=ALU.mult,
-            )
-
-        def scale_turned(j, g):
-            scale_pass(j, g, banks["x", j][:].bitcast(BF16)[:, g * BANK : (g + 1) * BANK])
-
-        def warm_tile():
-            nc.vector.memset(warm_operand[:].bitcast(I32), 0)
-
-        def warm(count):
-            bank = new_bank("warm")
-            for i in range(count):
-                nc.tensor.matmul(bank[:], lhsT=warm_operand[:, 0:P], rhs=warm_operand[:], start=True, stop=True)
 
         def widen_first(g):
             nc.vector.tensor_copy(out=first_wide[g][:], in_=x_raw[0][:, g * BANK : (g + 1) * BANK])
@@ -209,29 +191,45 @@ def tile_moslorasubspacemixerrankgain_w4_kernel(
             bank = new_bank("first", g)
             pairs = first_wide[g][:].bitcast(F32)
             for u in range(2):
-                nc.tensor.transpose(bank[:, u * P : (u + 1) * P], pairs[:, u:256:2], ident[:])
+                nc.tensor.transpose(bank[:, u * P : (u + 1) * P], pairs[:, u : BANK // 2 : 2], ident[:])
+
+        def scale_turned(j, g, turned):
+            lo = (2 * g + j % 2) * BANK
+            nc.vector.tensor_tensor(
+                out=x_turned[j // 2][:, lo : lo + BANK].rearrange("p (n u v) -> p n u v", u=2, v=2),
+                in0=turned.rearrange("p (u n v) -> p n u v", u=2, v=2),
+                in1=x_scale_cols[:, g * SLOTS : (g + 1) * SLOTS]
+                .rearrange("p (u v) -> p u v", u=2)
+                .unsqueeze(1)
+                .to_broadcast([P, P, 2, 2]),
+                op=ALU.mult,
+            )
 
         def scale_first(g):
-            scale_pass(0, g, banks["first", g][:].bitcast(BF16)[:, 0:BANK])
+            scale_turned(0, g, banks["first", g][:].bitcast(BF16)[:, 0:BANK])
 
-        def quant_x(first, count, g):
-            cols = slice((first % 4) * P, (first % 4 + count) * P)
-            nc.vector.quantize_mx(
-                out=x_codes[first // 4, g][:, cols].bitcast(FP8X4),
-                scales=x_scales[first // 4, g][:, cols],
-                in_=x_turned[first // 2][:, (2 * g + first % 2) * BANK : (2 * g + first % 2 + count) * BANK],
-            )
+        def scale_second(g):
+            scale_turned(1, g, banks["x", 1][:].bitcast(BF16)[:, g * BANK : (g + 1) * BANK])
+
+        def quant_x(first, count):
+            for g in range(PASSES):
+                lo = (2 * g + first % 2) * BANK
+                nc.vector.quantize_mx(
+                    out=x_codes[first // TILES_A_CHUNK, g][:, tile_cols(first, count)].bitcast(FP8X4),
+                    scales=x_scales[first // TILES_A_CHUNK, g][:, tile_cols(first, count)],
+                    in_=x_turned[first // 2][:, lo : lo + count * BANK],
+                )
 
         def base_mm(j, h):
             bank = new_bank("base", j, h)
-            cols = slice((j % 4) * P, (j % 4 + 1) * P)
             for g in range(PASSES):
+                lo = g * F + h * BANK
                 nc.tensor.matmul_mx(
                     out=bank[:],
-                    lhsT=x_codes[j // 4, g][:, cols].bitcast(FP8X4),
-                    lhsT_scale=x_scales[j // 4, g][:, cols],
-                    rhs=words["w0"][:, 2 * (g * F + h * BANK) : 2 * (g * F + (h + 1) * BANK)].bitcast(FP4X4),
-                    rhs_scale=scales["w0"][:, g * F + h * BANK : g * F + (h + 1) * BANK],
+                    lhsT=x_codes[j // TILES_A_CHUNK, g][:, tile_cols(j)].bitcast(FP8X4),
+                    lhsT_scale=x_scales[j // TILES_A_CHUNK, g][:, tile_cols(j)],
+                    rhs=words["w0"][:, 2 * lo : 2 * (lo + BANK)].bitcast(FP4X4),
+                    rhs_scale=scales["w0"][:, lo : lo + BANK],
                     start=(g == 0),
                     stop=(g == PASSES - 1),
                 )
@@ -263,20 +261,22 @@ def tile_moslorasubspacemixerrankgain_w4_kernel(
 
         def weave(planes, woven, s, copy):
             copy(
-                out=woven[:, s * 1024 : (s + 1) * 1024].rearrange("p (n i t) -> p n t i", i=4, t=PACK),
+                out=woven[:, s * SLOTS * PIECE : (s + 1) * SLOTS * PIECE].rearrange(
+                    "p (n i t) -> p n t i", i=4, t=SLOTS
+                ),
                 in_=planes[:]
-                .rearrange("p (t n) -> p t n", t=PACK)[:, :, s * 256 : (s + 1) * 256]
+                .rearrange("p (t n) -> p t n", t=SLOTS)[:, :, s * PIECE : (s + 1) * PIECE]
                 .rearrange("p t (n i) -> p n t i", i=4),
             )
 
-        def weave_p(c, s):
-            weave(pg_planes[c], pg_woven[c], s, on_vector)
+        def weave_pg(c, s):
+            weave(pg_planes[c], pg_woven[c], s, nc.vector.tensor_copy)
 
-        def quant_p(c, s):
+        def quant_pg(c, s):
             nc.vector.quantize_mx(
-                out=pg_codes[c][:, s * 256 : (s + 1) * 256].bitcast(FP8X4),
-                scales=pg_scales[c][:, s * 256 : (s + 1) * 256],
-                in_=pg_woven[c][:, s * 1024 : (s + 1) * 1024],
+                out=pg_codes[c][:, s * PIECE : (s + 1) * PIECE].bitcast(FP8X4),
+                scales=pg_scales[c][:, s * PIECE : (s + 1) * PIECE],
+                in_=pg_woven[c][:, s * SLOTS * PIECE : (s + 1) * SLOTS * PIECE],
             )
 
         def mix_mm(h, t):
@@ -302,11 +302,10 @@ def tile_moslorasubspacemixerrankgain_w4_kernel(
 
         def up_mm(j, h):
             bank = new_bank("up", j, h)
-            cols = slice((j % 4) * P, (j % 4 + 1) * P)
             nc.tensor.matmul_mx(
                 out=bank[:],
-                lhsT=pg_codes[j // 4][:, cols].bitcast(FP8X4),
-                lhsT_scale=pg_scales[j // 4][:, cols],
+                lhsT=pg_codes[j // TILES_A_CHUNK][:, tile_cols(j)].bitcast(FP8X4),
+                lhsT_scale=pg_scales[j // TILES_A_CHUNK][:, tile_cols(j)],
                 rhs=c_codes[h][:].bitcast(FP8X4),
                 rhs_scale=c_scales[h][:],
                 start=True,
@@ -322,65 +321,69 @@ def tile_moslorasubspacemixerrankgain_w4_kernel(
                 op0=ALU.mult,
                 op1=ALU.add,
             )
-
-        def store(j, h, lo=0, hi=BANK):
             nc.sync.dma_start(
                 out=out_rows[j // 2][j % 2][:, h * BANK + lo : h * BANK + hi], in_=result[j, h][:, lo:hi]
             )
 
-        clear_scales("m",nc.gpsimd)
-        clear_scales("bu",nc.gpsimd)
-        warm_tile()
-        clear_scales("w0",nc.vector)
-        clear_scales("a",nc.vector)
-        setup()
-        load_x(0,1)
+        def both(step, j):
+            for h in range(HALVES):
+                step(j, h)
+
+
+        clear_scales("m", nc.gpsimd)
+        clear_scales("bu", nc.gpsimd)
+        nc.vector.memset(warm_operand[:].bitcast(I32), 0)
+        clear_scales("w0", nc.vector)
+        clear_scales("a", nc.vector)
+        make_identity(nc, ident[:])
+        nc.gpsimd.memset(gain_square[:], 0.0)
+        load_x(0, 1)
         load_x_scale()
-        load_x(1,1)
-        load_words("m")
-        load_scales("m")
-        load_words("bu")
-        load_scales("bu")
-        load_x(2,2)
+        load_x(1, 1)
+        for w in ("m", "bu"):
+            load_words(w)
+            load_scales(w)
+        load_x(2, 2)
         load_words("w0")
         load_gain()
         load_scales("w0")
-        load_x(4,4)
+        load_x(4, 4)
         load_words("a")
         load_scales("a")
+
         warm(3)
-        widen_first(0)
-        widen_first(1)
-        widen_x(1,on_scalar_act)
-        turn_first(0)
-        turn_first(1)
+        for g in range(PASSES):
+            widen_first(g)
+        nc.scalar.activation(out=x_wide[1][:], in_=x_raw[1], func=ACT.Copy)
+        for g in range(PASSES):
+            turn_first(g)
+        warm(2)
         spread_mm(0)
-        spread_mm(1)
         turn_x(1)
-        warm(1)
-        scale_first(0)
-        scale_first(1)
+        spread_mm(1)
+        for g in range(PASSES):
+            scale_first(g)
         regroup("m")
-        spread_out(0,on_scalar)
-        spread_out(1,on_scalar)
-        widen_gain()
-        scale_turned(1,0)
-        quant_x(0,1,0)
-        quant_x(0,1,1)
-        scale_turned(1,1)
-        for t in range(4):
-            mix_mm(0,t)
-            mix_out(0,t)
+        for g in range(PASSES):
+            spread_out(g)
+        scale_second(0)
+        quant_x(0, 1)
+        scale_second(1)
+
+        for t in range(SLOTS):
+            mix_mm(0, t)
+            mix_out(0, t)
         scale_x(2)
-        quant_x(1,1,0)
-        quant_x(1,1,1)
+        quant_x(1, 1)
         scale_x(3)
-        for t in range(4):
-            mix_mm(1,t)
-        base_mm(0,0)
-        mix_out(1,0)
-        mix_out(1,1)
-        base_mm(0,1)
+        for t in range(SLOTS):
+            mix_mm(1, t)
+        base_mm(0, 0)
+        widen_gain()
+        mix_out(1, 0)
+        mix_out(1, 1)
+        base_mm(0, 1)
+
         turn_x(2)
         turn_x(3)
         turn_gain()
@@ -388,128 +391,89 @@ def tile_moslorasubspacemixerrankgain_w4_kernel(
         empty_x(3)
         empty_gain()
         scale_x(4)
-        regroup("a")
         scale_x(5)
-        quant_x(2,2,0)
-        quant_x(2,2,1)
+        regroup("a")
+        quant_x(2, 2)
         scale_x(6)
-        base_mm(1,0)
-        mix_out(1,2)
-        mix_out(1,3)
-        base_mm(1,1)
+        base_mm(1, 0)
+        mix_out(1, 2)
+        mix_out(1, 3)
+        base_mm(1, 1)
+
         turn_x(4)
         turn_x(5)
-        base_out(0,0)
+        base_out(0, 0)
         empty_x(4)
         empty_x(5)
-        down_mm(0,0)
-        down_mm(0,1)
-        down_out(0,0)
-        down_out(0,1)
+        for t in (0, 1):
+            down_mm(0, t)
+        for t in (0, 1):
+            down_out(0, t)
         scale_x(7)
-        weave_c(0,0,on_vector)
-        quant_x(4,2,0)
-        quant_x(4,2,1)
-        weave_c(0,1,on_vector)
-        down_mm(0,2)
+        weave_c(0, 0, nc.vector.tensor_copy)
+        quant_x(4, 2)
+        weave_c(0, 1, nc.vector.tensor_copy)
+        down_mm(0, 2)
+
         turn_x(6)
         turn_x(7)
-        down_out(0,2)
+        down_out(0, 2)
         empty_x(6)
         empty_x(7)
-        down_mm(0,3)
-        down_out(0,3)
-        weave_c(1,0,on_vector)
-        quant_x(6,2,0)
-        quant_x(6,2,1)
+        down_mm(0, 3)
+        down_out(0, 3)
+
+        weave_c(1, 0, nc.vector.tensor_copy)
+        quant_x(6, 2)
         quant_c(0)
-        base_mm(2,0)
-        base_mm(2,1)
-        base_out(0,1)
-        weave_c(1,1,on_scalar)
-        base_out(1,0)
-        weave_p(0,0)
-        weave_p(0,1)
-        quant_p(0,0)
+        both(base_mm, 2)
+        base_out(0, 1)
+        weave_c(1, 1, nc.scalar.copy)
+        base_out(1, 0)
+        weave_pg(0, 0)
+        weave_pg(0, 1)
+        quant_pg(0, 0)
         quant_c(1)
-        quant_p(0,1)
-        base_mm(3,0)
-        for t in range(4):
-            down_mm(1,t)
-            down_out(1,t)
-        base_out(1,1)
-        base_out(2,0)
-        base_out(2,1)
-        up_mm(0,0)
-        up_mm(0,1)
-        up_mm(1,0)
-        finish(0,0)
-        store(0,0)
-        finish(0,1)
-        store(0,1)
-        base_mm(3,1)
-        up_mm(1,1)
-        base_out(3,0)
-        base_out(3,1)
-        weave_p(1,0)
-        finish(1,0)
-        store(1,0)
-        weave_p(1,1)
-        finish(1,1)
-        store(1,1)
-        quant_p(1,0)
-        up_mm(2,0)
-        up_mm(2,1)
-        base_mm(4,0)
-        base_mm(4,1)
-        base_out(4,0)
-        base_out(4,1)
-        finish(2,0)
-        store(2,0)
-        quant_p(1,1)
-        finish(2,1)
-        store(2,1)
-        up_mm(3,0)
-        up_mm(3,1)
-        base_mm(5,0)
-        base_mm(5,1)
-        base_out(5,0)
-        base_out(5,1)
-        finish(3,0)
-        store(3,0)
-        finish(3,1)
-        store(3,1)
-        up_mm(4,0)
-        up_mm(4,1)
-        base_mm(6,0)
-        base_mm(6,1)
-        base_out(6,0)
-        base_out(6,1)
-        finish(4,0)
-        store(4,0)
-        finish(4,1)
-        store(4,1)
-        up_mm(5,0)
-        up_mm(5,1)
-        base_mm(7,0)
-        up_mm(6,0)
-        base_mm(7,1)
-        base_out(7,0)
-        base_out(7,1)
-        finish(5,0)
-        store(5,0)
-        finish(5,1)
-        store(5,1)
-        up_mm(6,1)
-        up_mm(7,0)
-        up_mm(7,1)
-        finish(6,0)
-        store(6,0)
-        finish(6,1)
-        store(6,1)
-        finish(7,0)
-        store(7,0)
-        finish(7,1,0,256)
-        store(7,1,0,256)
-        finish(7,1,256,512)
-        store(7,1,256,512)
+        quant_pg(0, 1)
+        base_mm(3, 0)
+        for t in range(SLOTS):
+            down_mm(1, t)
+            down_out(1, t)
+        base_out(1, 1)
+        both(base_out, 2)
+
+        both(up_mm, 0)
+        up_mm(1, 0)
+        both(finish, 0)
+        base_mm(3, 1)
+        up_mm(1, 1)
+        both(base_out, 3)
+        weave_pg(1, 0)
+        finish(1, 0)
+        quant_pg(1, 0)
+        finish(1, 1)
+        for j in (2, 3):
+            both(up_mm, j)
+            both(base_mm, j + 2)
+            both(base_out, j + 2)
+            both(finish, j)
+        both(up_mm, 4)
+        both(base_mm, 6)
+        both(base_out, 6)
+        finish(4, 0)
+        weave_pg(1, 1)
+        finish(4, 1)
+        quant_pg(1, 1)
+
+        both(up_mm, 5)
+        base_mm(7, 0)
+        up_mm(6, 0)
+        base_mm(7, 1)
+        both(base_out, 7)
+        both(finish, 5)
+        up_mm(6, 1)
+        both(up_mm, 7)
+        both(finish, 6)
+        finish(7, 0)
+        finish(7, 1, 0, BANK // 2)
+        finish(7, 1, BANK // 2, BANK)

import math
from contextlib import ExitStack

import concourse.mybir as mybir
from concourse.masks import make_identity

N, D, F, R = 1024, 1024, 1024, 512
FLOPS = 2 * N * D * F + 2 * N * D * R + 2 * R * R * F + 2 * N * R * F

F32 = mybir.dt.float32
BF16 = mybir.dt.bfloat16
I32 = mybir.dt.int32
U32 = mybir.dt.uint32
U8 = mybir.dt.uint8
FP8 = mybir.dt.float8_e4m3fn
FP8X4 = mybir.dt.float8_e4m3fn_x4
FP4X4 = mybir.dt.float4_e2m1fn_x4
ALU = mybir.AluOpType
ACT = mybir.ActivationFunctionType

P = 128
SLOTS = 4
BANK = 512
PSUM_BANKS = 8
TILES = N // P
PASSES = D // BANK
CHUNKS = N // BANK
TILES_A_CHUNK = TILES // CHUNKS
HALVES = F // BANK
QUADRANTS = 4
GROUPS = 16
PIECE = 256


def tile_moslorasubspacemixerrankgain_w4_kernel(
    tc, x_bytes, x_scale, w0_words, w0_scales, a_words, a_scales, d, m_words, m_scales, bu_words, bu_scales, out
):
    nc = tc.nc
    with ExitStack() as ctx:
        keep = ctx.enter_context(tc.tile_pool(name="keep", bufs=1))
        psum = ctx.enter_context(tc.psum_pool(name="psum", bufs=PSUM_BANKS))
        ctx.enter_context(tc.manual_schedule())

        def sb(name, cols, dtype, rows=P):
            return keep.tile([rows, cols], dtype, name=name, align_bytes=64)

        hbm_words = {"w0": w0_words, "a": a_words, "m": m_words, "bu": bu_words}
        hbm_scales = {"w0": w0_scales, "a": a_scales, "m": m_scales, "bu": bu_scales}
        scales = {w: sb(w + "_scale_rows", s.shape[0] * s.shape[2], U8) for w, s in hbm_scales.items()}
        words = {w: sb(w + "_code_words", s.shape[0] * s.shape[2], U8) for w, s in hbm_words.items()}
        sliced_words = {w: sb(w + "_sliced_words", words[w].shape[1], U8) for w in ("a", "m")}
        sliced_scales = {w: sb(w + "_sliced_scales", scales[w].shape[1], U8) for w in ("a", "m")}

        ident = sb("ident", P, F32)
        gain_rows = sb("gain_rows", P, BF16, rows=SLOTS)
        gain_square = sb("gain_square", P, F32)
        gain = sb("gain", SLOTS, F32)
        x_scale_cols = sb("x_scale_cols", PASSES * SLOTS, F32)
        x_scale_spread = sb("x_scale_spread", D, F32)

        x_rows = x_bytes.rearrange("(h n e) k -> h n (e k)", n=P, e=2)
        out_rows = out.rearrange("(h n e) f -> h e n f", n=P, e=2)
        x_raw = {}
        x_wide = {j: sb("x_wide_%d" % j, D, BF16) for j in range(1, TILES)}
        x_turned = [sb("x_turned_%d" % i, 2 * D, BF16) for i in range(TILES // 2)]
        first_wide = [sb("first_wide_%d" % g, BANK, BF16) for g in range(PASSES)]
        warm_operand = sb("warm_operand", BANK, BF16)
        x_codes = {(c, g): sb("x_codes_%d_%d" % (c, g), BANK, U32) for c in range(CHUNKS) for g in range(PASSES)}
        x_scales = {(c, g): sb("x_scales_%d_%d" % (c, g), BANK, U8) for c in range(CHUNKS) for g in range(PASSES)}
        pg_planes = [sb("pg_planes_%d" % c, SLOTS * BANK, BF16) for c in range(CHUNKS)]
        pg_woven = [sb("pg_woven_%d" % c, SLOTS * BANK, BF16) for c in range(CHUNKS)]
        pg_codes = [sb("pg_codes_%d" % c, BANK, U32) for c in range(CHUNKS)]
        pg_scales = [sb("pg_scales_%d" % c, BANK, U8) for c in range(CHUNKS)]
        c_planes = [sb("c_planes_%d" % h, SLOTS * BANK, BF16) for h in range(HALVES)]
        c_woven = [sb("c_woven_%d" % h, SLOTS * BANK, BF16) for h in range(HALVES)]
        c_codes = [sb("c_codes_%d" % h, BANK, U32) for h in range(HALVES)]
        c_scales = [sb("c_scales_%d" % h, BANK, U8) for h in range(HALVES)]
        result = {(j, h): sb("result_%d_%d" % (j, h), BANK, F32) for j in range(TILES) for h in range(HALVES)}
        banks = {}

        def new_bank(*key):
            banks[key] = psum.tile([P, BANK], F32, name="bank", tag="bank")
            return banks[key]

        def tile_cols(j, count=1):
            return slice((j % TILES_A_CHUNK) * P, (j % TILES_A_CHUNK + count) * P)

        def clear_scales(w, engine):
            engine.memset(scales[w][:].bitcast(I32), 0)

        def load_x_scale():
            nc.sync.dma_start(
                out=x_scale_cols[:].rearrange("p (g t) -> p g t", t=SLOTS),
                in_=x_scale.rearrange("o (g p t) -> p (o g) t", p=P, t=SLOTS),
            )

        def load_x(first, count):
            raw = sb("x_raw_%d" % first, count * D, U8)
            if count == 1:
                lo = (first % 2) * D
                nc.sync.dma_start(out=raw[:], in_=x_rows[first // 2][:, lo : lo + D])
            else:
                nc.sync.dma_start(
                    out=raw[:].rearrange("n (h c) -> n h c", c=2 * D),
                    in_=x_rows[first // 2 : (first + count) // 2].rearrange("h n c -> n h c"),
                )
            for i in range(count):
                x_raw[first + i] = raw[:, i * D : (i + 1) * D].bitcast(FP8)

        def load_words(w):
            passes = hbm_words[w].shape[0]
            nc.sync.dma_start(
                out=words[w][:].bitcast(I32).rearrange("p (g n) -> p g n", g=passes),
                in_=hbm_words[w].bitcast(I32).rearrange("g p n -> p g n"),
            )

        def load_scales(w):
            passes = hbm_scales[w].shape[0]
            for quad in range(QUADRANTS):
                nc.sync.dma_start(
                    out=scales[w][32 * quad : 32 * quad + 4, :].bitcast(I32).rearrange("p (g n) -> p g n", g=passes),
                    in_=hbm_scales[w][:, 4 * quad : 4 * quad + 4, :].bitcast(I32).rearrange("g j n -> j g n"),
                )

        def load_gain():
            nc.sync.dma_start(
                out=gain_rows[:].rearrange("t (q i) -> t q i", i=8),
                in_=d.rearrange("(q t i) -> t q i", t=SLOTS, i=8),
            )

        def widen_gain():
            nc.scalar.copy(out=gain_square[0:SLOTS, :], in_=gain_rows[:])

        def turn_gain():
            bank = new_bank("gain")
            nc.tensor.transpose(bank[:, 0:P], gain_square[:], ident[:])

        def empty_gain():
            nc.scalar.copy(out=gain[:], in_=banks["gain",][:, 0:SLOTS])

        def regroup(w):
            for src, dst, run in ((words[w], sliced_words[w], 4), (scales[w], sliced_scales[w], 2)):
                nc.vector.tensor_copy(
                    out=dst[:].bitcast(I32).rearrange("p (g t q i) -> p g t q i", t=SLOTS, q=GROUPS, i=run),
                    in_=src[:].bitcast(I32).rearrange("p (g q t i) -> p g t q i", t=SLOTS, q=GROUPS, i=run),
                )

        def spread_mm(g):
            bank = new_bank("spread", g)
            for t in range(SLOTS):
                col = g * SLOTS + t
                nc.tensor.transpose(
                    bank[:, t * P : (t + 1) * P], x_scale_cols[:, col : col + 1].to_broadcast([P, P]), ident[:]
                )

        def spread_out(g):
            nc.scalar.copy(
                out=x_scale_spread[:, g * BANK : (g + 1) * BANK].rearrange("q (p t) -> q p t", t=SLOTS),
                in_=banks["spread", g][:].rearrange("q (t p) -> q p t", t=SLOTS),
            )

        def warm(count):
            bank = new_bank("warm")
            for repeat in range(count):
                nc.tensor.matmul(bank[:], lhsT=warm_operand[:, 0:P], rhs=warm_operand[:], start=True, stop=True)

        def scale_x(j):
            nc.vector.tensor_tensor(out=x_wide[j][:], in0=x_raw[j], in1=x_scale_spread[:], op=ALU.mult)

        def turn_x(j):
            bank = new_bank("x", j)
            pairs = x_wide[j][:].bitcast(F32)
            half = BANK // 2
            for g in range(PASSES):
                for u in range(2):
                    lo = (2 * g + u) * P
                    nc.tensor.transpose(bank[:, lo : lo + P], pairs[:, half * g + u : half * (g + 1) : 2], ident[:])

        def empty_x(j):
            nc.scalar.copy(
                out=x_turned[j // 2][:].bitcast(F32).rearrange("p (g e n u) -> p g e n u", g=PASSES, e=2, u=2)[
                    :, :, j % 2
                ],
                in_=banks["x", j][:].rearrange("p (g u n) -> p g n u", g=PASSES, u=2),
            )

        def widen_first(g):
            nc.vector.tensor_copy(out=first_wide[g][:], in_=x_raw[0][:, g * BANK : (g + 1) * BANK])

        def turn_first(g):
            bank = new_bank("first", g)
            pairs = first_wide[g][:].bitcast(F32)
            for u in range(2):
                nc.tensor.transpose(bank[:, u * P : (u + 1) * P], pairs[:, u : BANK // 2 : 2], ident[:])

        def scale_turned(j, g, turned):
            lo = (2 * g + j % 2) * BANK
            nc.vector.tensor_tensor(
                out=x_turned[j // 2][:, lo : lo + BANK].rearrange("p (n u v) -> p n u v", u=2, v=2),
                in0=turned.rearrange("p (u n v) -> p n u v", u=2, v=2),
                in1=x_scale_cols[:, g * SLOTS : (g + 1) * SLOTS]
                .rearrange("p (u v) -> p u v", u=2)
                .unsqueeze(1)
                .to_broadcast([P, P, 2, 2]),
                op=ALU.mult,
            )

        def scale_first(g):
            scale_turned(0, g, banks["first", g][:].bitcast(BF16)[:, 0:BANK])

        def scale_second(g):
            scale_turned(1, g, banks["x", 1][:].bitcast(BF16)[:, g * BANK : (g + 1) * BANK])

        def quant_x(first, count):
            for g in range(PASSES):
                lo = (2 * g + first % 2) * BANK
                nc.vector.quantize_mx(
                    out=x_codes[first // TILES_A_CHUNK, g][:, tile_cols(first, count)].bitcast(FP8X4),
                    scales=x_scales[first // TILES_A_CHUNK, g][:, tile_cols(first, count)],
                    in_=x_turned[first // 2][:, lo : lo + count * BANK],
                )

        def base_mm(j, h):
            bank = new_bank("base", j, h)
            for g in range(PASSES):
                lo = g * F + h * BANK
                nc.tensor.matmul_mx(
                    out=bank[:],
                    lhsT=x_codes[j // TILES_A_CHUNK, g][:, tile_cols(j)].bitcast(FP8X4),
                    lhsT_scale=x_scales[j // TILES_A_CHUNK, g][:, tile_cols(j)],
                    rhs=words["w0"][:, 2 * lo : 2 * (lo + BANK)].bitcast(FP4X4),
                    rhs_scale=scales["w0"][:, lo : lo + BANK],
                    start=(g == 0),
                    stop=(g == PASSES - 1),
                )

        def base_out(j, h):
            nc.scalar.copy(out=result[j, h][:], in_=banks["base", j, h][:])

        def down_mm(c, t):
            bank = new_bank("down", c, t)
            for g in range(PASSES):
                lo = g * R + t * P
                nc.tensor.matmul_mx(
                    out=bank[:],
                    lhsT=sliced_words["a"][:, 2 * lo : 2 * (lo + P)].bitcast(FP4X4),
                    lhsT_scale=sliced_scales["a"][:, lo : lo + P],
                    rhs=x_codes[c, g][:].bitcast(FP8X4),
                    rhs_scale=x_scales[c, g][:],
                    start=(g == 0),
                    stop=(g == PASSES - 1),
                )

        def down_out(c, t):
            nc.scalar.activation(
                out=pg_planes[c][:, t * BANK : (t + 1) * BANK],
                in_=banks["down", c, t][:],
                func=ACT.Copy,
                scale=gain[:, t : t + 1],
            )

        def weave(planes, woven, s, copy):
            copy(
                out=woven[:, s * SLOTS * PIECE : (s + 1) * SLOTS * PIECE].rearrange(
                    "p (n i t) -> p n t i", i=4, t=SLOTS
                ),
                in_=planes[:]
                .rearrange("p (t n) -> p t n", t=SLOTS)[:, :, s * PIECE : (s + 1) * PIECE]
                .rearrange("p t (n i) -> p n t i", i=4),
            )

        def weave_pg(c, s):
            weave(pg_planes[c], pg_woven[c], s, nc.vector.tensor_copy)

        def quant_pg(c, s):
            nc.vector.quantize_mx(
                out=pg_codes[c][:, s * PIECE : (s + 1) * PIECE].bitcast(FP8X4),
                scales=pg_scales[c][:, s * PIECE : (s + 1) * PIECE],
                in_=pg_woven[c][:, s * SLOTS * PIECE : (s + 1) * SLOTS * PIECE],
            )

        def mix_mm(h, t):
            bank = new_bank("mix", h, t)
            nc.tensor.matmul_mx(
                out=bank[:],
                lhsT=sliced_words["m"][:, 2 * t * P : 2 * (t + 1) * P].bitcast(FP4X4),
                lhsT_scale=sliced_scales["m"][:, t * P : (t + 1) * P],
                rhs=words["bu"][:, 2 * h * BANK : 2 * (h + 1) * BANK].bitcast(FP4X4),
                rhs_scale=scales["bu"][:, h * BANK : (h + 1) * BANK],
                start=True,
                stop=True,
            )

        def mix_out(h, t):
            nc.scalar.copy(out=c_planes[h][:, t * BANK : (t + 1) * BANK], in_=banks["mix", h, t][:])

        def weave_c(h, s, copy):
            weave(c_planes[h], c_woven[h], s, copy)

        def quant_c(h):
            nc.vector.quantize_mx(out=c_codes[h][:].bitcast(FP8X4), scales=c_scales[h][:], in_=c_woven[h][:])

        def up_mm(j, h):
            bank = new_bank("up", j, h)
            nc.tensor.matmul_mx(
                out=bank[:],
                lhsT=pg_codes[j // TILES_A_CHUNK][:, tile_cols(j)].bitcast(FP8X4),
                lhsT_scale=pg_scales[j // TILES_A_CHUNK][:, tile_cols(j)],
                rhs=c_codes[h][:].bitcast(FP8X4),
                rhs_scale=c_scales[h][:],
                start=True,
                stop=True,
            )

        def finish(j, h, lo=0, hi=BANK):
            nc.vector.scalar_tensor_tensor(
                out=result[j, h][:, lo:hi],
                in0=banks["up", j, h][:, lo:hi],
                scalar=1.0 / math.sqrt(R),
                in1=result[j, h][:, lo:hi],
                op0=ALU.mult,
                op1=ALU.add,
            )
            nc.sync.dma_start(
                out=out_rows[j // 2][j % 2][:, h * BANK + lo : h * BANK + hi], in_=result[j, h][:, lo:hi]
            )

        def both(step, j):
            for h in range(HALVES):
                step(j, h)


        clear_scales("m", nc.gpsimd)
        clear_scales("bu", nc.gpsimd)
        nc.vector.memset(warm_operand[:].bitcast(I32), 0)
        clear_scales("w0", nc.vector)
        clear_scales("a", nc.vector)
        make_identity(nc, ident[:])
        nc.gpsimd.memset(gain_square[:], 0.0)
        load_x(0, 1)
        load_x_scale()
        load_x(1, 1)
        for w in ("m", "bu"):
            load_words(w)
            load_scales(w)
        load_x(2, 2)
        load_words("w0")
        load_gain()
        load_scales("w0")
        load_x(4, 4)
        load_words("a")
        load_scales("a")

        warm(3)
        for g in range(PASSES):
            widen_first(g)
        nc.scalar.activation(out=x_wide[1][:], in_=x_raw[1], func=ACT.Copy)
        for g in range(PASSES):
            turn_first(g)
        warm(2)
        spread_mm(0)
        turn_x(1)
        spread_mm(1)
        for g in range(PASSES):
            scale_first(g)
        regroup("m")
        for g in range(PASSES):
            spread_out(g)
        scale_second(0)
        quant_x(0, 1)
        scale_second(1)

        for t in range(SLOTS):
            mix_mm(0, t)
            mix_out(0, t)
        scale_x(2)
        quant_x(1, 1)
        scale_x(3)
        for t in range(SLOTS):
            mix_mm(1, t)
        base_mm(0, 0)
        widen_gain()
        mix_out(1, 0)
        mix_out(1, 1)
        base_mm(0, 1)

        turn_x(2)
        turn_x(3)
        turn_gain()
        empty_x(2)
        empty_x(3)
        empty_gain()
        scale_x(4)
        scale_x(5)
        regroup("a")
        quant_x(2, 2)
        scale_x(6)
        base_mm(1, 0)
        mix_out(1, 2)
        mix_out(1, 3)
        base_mm(1, 1)

        turn_x(4)
        turn_x(5)
        base_out(0, 0)
        empty_x(4)
        empty_x(5)
        for t in (0, 1):
            down_mm(0, t)
        for t in (0, 1):
            down_out(0, t)
        scale_x(7)
        weave_c(0, 0, nc.vector.tensor_copy)
        quant_x(4, 2)
        weave_c(0, 1, nc.vector.tensor_copy)
        down_mm(0, 2)

        turn_x(6)
        turn_x(7)
        down_out(0, 2)
        empty_x(6)
        empty_x(7)
        down_mm(0, 3)
        down_out(0, 3)

        weave_c(1, 0, nc.vector.tensor_copy)
        quant_x(6, 2)
        quant_c(0)
        both(base_mm, 2)
        base_out(0, 1)
        weave_c(1, 1, nc.scalar.copy)
        base_out(1, 0)
        weave_pg(0, 0)
        weave_pg(0, 1)
        quant_pg(0, 0)
        quant_c(1)
        quant_pg(0, 1)
        base_mm(3, 0)
        for t in range(SLOTS):
            down_mm(1, t)
            down_out(1, t)
        base_out(1, 1)
        both(base_out, 2)

        both(up_mm, 0)
        up_mm(1, 0)
        both(finish, 0)
        base_mm(3, 1)
        up_mm(1, 1)
        both(base_out, 3)
        weave_pg(1, 0)
        finish(1, 0)
        quant_pg(1, 0)
        finish(1, 1)
        for j in (2, 3):
            both(up_mm, j)
            both(base_mm, j + 2)
            both(base_out, j + 2)
            both(finish, j)
        both(up_mm, 4)
        both(base_mm, 6)
        both(base_out, 6)
        finish(4, 0)
        weave_pg(1, 1)
        finish(4, 1)
        quant_pg(1, 1)

        both(up_mm, 5)
        base_mm(7, 0)
        up_mm(6, 0)
        base_mm(7, 1)
        both(base_out, 7)
        both(finish, 5)
        up_mm(6, 1)
        both(up_mm, 7)
        both(finish, 6)
        finish(7, 0)
        finish(7, 1, 0, BANK // 2)
        finish(7, 1, BANK // 2, BANK)
